import numpy as np
import ml_dtypes


def mxq(x, axis, fmt="e4m3"):
    dtype, down = {"e4m3": (ml_dtypes.float8_e4m3fn, 7), "e5m2": (ml_dtypes.float8_e5m2, 14)}[fmt]
    v = np.moveaxis(np.asarray(x, np.float32).astype(ml_dtypes.bfloat16).astype(np.float64), axis, -1)
    blocks = v.reshape(v.shape[:-1] + (-1, 32))
    amax = np.abs(blocks).max(-1, keepdims=True)
    byte = np.maximum(np.where(amax > 0, np.frexp(amax)[1] - 1 + 127, 0) - down, 1)
    scale = np.exp2(byte - 127.0)
    codes = (blocks / scale).astype(np.float32).astype(dtype).astype(np.float64)
    return np.moveaxis((codes * scale).reshape(v.shape), -1, axis)


WIDE = False


def mx_kscale(k):
    if not WIDE:
        return np.ones(k)
    levels = np.array([10, -10, 5, -5, 0])
    if k % 512:
        return np.exp2(np.random.permutation(np.resize(levels, k // 32))).repeat(32)
    a = np.empty((k // 512, 16))
    for p in range(k // 512):
        a[p, :8] = np.random.permutation(np.resize(levels, 8))
        for g in range(8):
            far = levels[np.abs(levels - a[p, g]) >= 10]
            a[p, g + 8] = far[np.random.randint(len(far))]
    return np.exp2(a.ravel()).repeat(32)


def f64(x):
    return np.asarray(x).astype(np.float64)


def striped(idx):
    return np.tile(idx.reshape(-1, 16).T, (8, 1)).astype(np.uint16)


def unstriped(offs):
    return offs[:16].T.reshape(-1).astype(np.int64)


K, T, D, V, H, N = 1536, 1024, 4, 512, 512, 256
P = 2 ** 7


def setup_inputs():
    n = np.random.standard_normal
    s = mx_kscale(K)[:, None]
    u = mx_kscale(H)
    return {
        "xT": (n((K, T)) * s).astype(np.float32),
        "w1": (n((K, H)) / np.sqrt(K) / s * u).astype(np.float32),
        "w2": (n((H, N)) / np.sqrt(H) / u[:, None]).astype(np.float32),
        "gate": np.tile(np.random.uniform(0.2, 1.0, (D, 1, V)) / np.sqrt(D), (1, P, 1)).astype(np.float32),
        "pos1": striped(np.random.permutation(T)[:V]),
        "pos2": striped(np.random.permutation(T)[:V]),
        "pos3": striped(np.random.permutation(T)[:V]),
        "pos4": striped(np.random.permutation(T)[:V]),
    }


def reference(xT, w1, w2, gate, pos1, pos2, pos3, pos4):
    h = mxq(f64(w1), 0, "e4m3").T @ mxq(f64(xT), 0, "e4m3")
    z = sum(f64(gate)[d, :1] * h[:, unstriped(p)] for d, p in enumerate((pos1, pos2, pos3, pos4)))
    return mxq(f64(w2), 0, "e4m3").T @ mxq(z, 0, "e4m3")

@@ -1,0 +1,254 @@
+from contextlib import ExitStack
+
+import concourse.mybir as mybir
+from concourse.masks import make_identity
+
+F32 = mybir.dt.float32
+BF16 = mybir.dt.bfloat16
+U32 = mybir.dt.uint32
+U16 = mybir.dt.uint16
+U8 = mybir.dt.uint8
+FP8X4 = mybir.dt.float8_e4m3fn_x4
+MULT = mybir.AluOpType.mult
+
+P = 128
+PACK = 4
+K, T, D, V, H, N = 1536, 1024, 4, 512, 512, 256
+K_PASS = P * PACK
+PASSES = K // K_PASS
+BLOCKS = H // P
+HALF = 512
+CHUNK = 128
+
+FLOPS = 2 * (K * H * T + H * N * V)
+
+
+def interleave(copy, dst, src):
+    copy(
+        out=dst.rearrange("p (c i) t -> p c t i", i=4),
+        in_=src.rearrange("p t (c i) -> p c t i", i=4),
+    )
+
+
+def tile_picked_gcn_mlp_none_sub_l_kernel(
+    tc, xT, w1, w2, gate, pos1, pos2, pos3, pos4, out
+):
+    nc = tc.nc
+    vcopy = nc.vector.tensor_copy
+    scopy = nc.scalar.copy
+
+    with ExitStack() as ctx:
+        keep = ctx.enter_context(tc.tile_pool(name="keep", bufs=1))
+        ring = ctx.enter_context(tc.tile_pool(name="ring", bufs=2))
+        hps = ctx.enter_context(tc.psum_pool(name="hps", bufs=4))
+        zps = ctx.enter_context(tc.psum_pool(name="zps", bufs=2))
+        tps = ctx.enter_context(tc.psum_pool(name="tps", bufs=2))
+
+        ident = keep.tile([P, P], F32, name="ident")
+        make_identity(nc, ident[:])
+
+        w1_raw = []
+        for b in range(BLOCKS):
+            w1_raw.append(keep.tile([P, PASSES, PACK, P], F32, name=f"w1_raw{b}"))
+        x_raw = []
+        for c in range(PASSES):
+            x_raw.append(keep.tile([P, PACK, T], F32, name=f"x_raw{c}"))
+        lists = []
+        for d in range(D):
+            lists.append(keep.tile([P, V // 16], U16, name=f"list{d}"))
+        gate_sb = keep.tile([P, D, V], F32, name="gate_sb")
+        w2_raw = keep.tile([P, PACK, N], F32, name="w2_raw")
+
+        def load_w1(b):
+            for c in range(PASSES):
+                nc.sync.dma_start(
+                    out=w1_raw[b][:, c],
+                    in_=w1[c * K_PASS : (c + 1) * K_PASS, b * P : (b + 1) * P].rearrange("(p j) n -> p j n", j=PACK),
+                )
+
+        def load_x(c, w0, w1_):
+            nc.sync.dma_start(
+                out=x_raw[c][:, :, w0:w1_],
+                in_=xT[c * K_PASS : (c + 1) * K_PASS, w0:w1_].rearrange("(p j) w -> p j w", j=PACK),
+            )
+
+        pieces = [(0, 0, 512), (0, 512, 1024), (1, 0, 512), (1, 512, 1024), (2, 0, 512), (2, 512, 768), (2, 768, 1024)]
+        load_w1(0)
+        for c, a, e in pieces[:4]:
+            load_x(c, a, e)
+        for tile, src in zip(lists, (pos1, pos2, pos3, pos4)):
+            nc.sync.dma_start(tile[:], src)
+        for c, a, e in pieces[4:]:
+            load_x(c, a, e)
+        nc.sync.dma_start(out=gate_sb[:, 0], in_=gate[0])
+        nc.sync.dma_start(out=gate_sb[:, 1], in_=gate[1])
+        load_w1(1)
+        nc.sync.dma_start(out=gate_sb[:, 2], in_=gate[2])
+        nc.sync.dma_start(out=gate_sb[:, 3], in_=gate[3])
+        load_w1(2)
+        load_w1(3)
+        nc.sync.dma_start(out=w2_raw[:], in_=w2.rearrange("(p j) m -> p j m", j=PACK))
+
+        x_bf, x_codes, x_scales = [], [], []
+        for c in range(PASSES):
+            x_bf.append(keep.tile([P, T, PACK], BF16, name=f"x_bf{c}", align_bytes=64))
+            x_codes.append(keep.tile([P, T], U32, name=f"x_codes{c}", align_bytes=64))
+            x_scales.append(keep.tile([P, T], U8, name=f"x_scales{c}", align_bytes=64))
+        w1_bf, w1_codes, w1_scales = [], [], []
+        for b in range(BLOCKS):
+            w1_bf.append(keep.tile([P, PASSES, P, PACK], BF16, name=f"w1_bf{b}", align_bytes=64))
+            w1_codes.append(keep.tile([P, PASSES, P], U32, name=f"w1_codes{b}", align_bytes=64))
+            w1_scales.append(keep.tile([P, PASSES, P], U8, name=f"w1_scales{b}", align_bytes=64))
+
+        def quantise(codes, scales, grouped):
+            nc.vector.quantize_mx(
+                out=codes.bitcast(FP8X4), scales=scales, in_=grouped.rearrange("p w t -> p (w t)")
+            )
+
+        def interleave_w1(b, copy):
+            for c in range(PASSES):
+                interleave(copy, w1_bf[b][:, c], w1_raw[b][:, c])
+
+        def quantise_w1(b, c0, c1):
+            nc.vector.quantize_mx(
+                out=w1_codes[b][:, c0:c1].rearrange("p c n -> p (c n)").bitcast(FP8X4),
+                scales=w1_scales[b][:, c0:c1].rearrange("p c n -> p (c n)"),
+                in_=w1_bf[b][:, c0:c1].rearrange("p c n t -> p (c n t)"),
+            )
+
+        def project(acc, b, c, a, e):
+            nc.tensor.matmul_mx(
+                out=acc,
+                lhsT=w1_codes[b][:, c].bitcast(FP8X4),
+                lhsT_scale=w1_scales[b][:, c],
+                rhs=x_codes[c][:, a:e].bitcast(FP8X4),
+                rhs_scale=x_scales[c][:, a:e],
+                start=(c == 0),
+                stop=(c == PASSES - 1),
+            )
+
+        interleave_w1(0, vcopy)
+        quantise_w1(0, 0, 2)
+        quantise_w1(0, 2, 3)
+        h = []
+        for b in range(BLOCKS):
+            h.append(keep.tile([P, T], F32, name=f"h{b}"))
+        groups = ((0, 512), (512, 768), (768, 1024))
+        accs = []
+        for a, e in groups:
+            accs.append(hps.tile([P, HALF], F32, name="acc"))
+        for c, a, e in pieces:
+            cut = a + (e - a) * 5 // 8
+            interleave(vcopy, x_bf[c][:, a:cut], x_raw[c][:, :, a:cut])
+            interleave(scopy, x_bf[c][:, cut:e], x_raw[c][:, :, cut:e])
+            quantise(x_codes[c][:, a:e], x_scales[c][:, a:e], x_bf[c][:, a:e])
+            for acc, (ga, ge) in zip(accs, groups):
+                if a <= ga and ge <= e:
+                    project(acc[:, 0 : ge - ga], 0, c, ga, ge)
+        scopy(out=h[0][:, 0:512], in_=accs[0][:])
+        scopy(out=h[0][:, 512:768], in_=accs[1][:, 0:256])
+        vcopy(out=h[0][:, 768:1024], in_=accs[2][:, 0:256])
+
+        w2_bf = keep.tile([P, N, PACK], BF16, name="w2_bf", align_bytes=64)
+        w2_codes = keep.tile([P, N], U32, name="w2_codes", align_bytes=64)
+        w2_scales = keep.tile([P, N], U8, name="w2_scales", align_bytes=64)
+
+        zT = keep.tile([P, V // CHUNK, PACK, P], F32, name="zT")
+        z_bf = keep.tile([P, V, PACK], BF16, name="z_bf", align_bytes=64)
+        z_codes = keep.tile([P, V], U32, name="z_codes", align_bytes=64)
+        z_scales = keep.tile([P, V], U8, name="z_scales", align_bytes=64)
+
+        def add_turned(dst, g, first):
+            for d in range(D):
+                nc.tensor.matmul(
+                    dst,
+                    g[:, d, first : first + CHUNK],
+                    ident[:],
+                    start=(d == 0),
+                    stop=(d == D - 1),
+                    is_transpose=True,
+                )
+
+        def gather(g, b, d, v0, v1):
+            offsets = lists[d][:, v0 // 16 : v1 // 16]
+            nc.vector.tensor_tensor(g[:, d], h[b][:].indirect(offsets), gate_sb[:, d, v0:v1], MULT)
+
+        for b in range(BLOCKS - 1):
+            nb = b + 1
+            interleave_w1(nb, scopy)
+            g = ring.tile([P, D, V], F32, name="g")
+            acc_a = hps.tile([P, HALF], F32, name="acc")
+            acc_b = hps.tile([P, HALF], F32, name="acc")
+            gather(g, b, 0, 0, V)
+            quantise_w1(nb, 0, 2)
+            for c in range(2):
+                project(acc_a[:], nb, c, 0, HALF)
+                project(acc_b[:], nb, c, HALF, T)
+            gather(g, b, 1, 0, V)
+            quantise_w1(nb, 2, 3)
+            project(acc_a[:], nb, 2, 0, HALF)
+            project(acc_b[:], nb, 2, HALF, T)
+            scopy(out=h[nb][:, 0:HALF], in_=acc_a[:])
+            scopy(out=h[nb][:, HALF:T], in_=acc_b[:])
+            gather(g, b, 2, 0, V)
+            if nb == BLOCKS - 1:
+                interleave(scopy, w2_bf[:], w2_raw[:])
+                quantise(w2_codes[:], w2_scales[:], w2_bf[:])
+            gather(g, b, 3, 0, V)
+            bank = zps.tile([P, V // CHUNK, P], F32, name="bank")
+            for s in range(V // CHUNK):
+                add_turned(bank[:, s], g, s * CHUNK)
+            scopy(
+                out=zT[:, :, :, b * 32 : (b + 1) * 32],
+                in_=bank[:].rearrange("v s (q t) -> v s t q", t=PACK),
+            )
+
+        b = BLOCKS - 1
+        chunks = V // CHUNK
+
+        def span(s):
+            return slice(s * CHUNK, (s + 1) * CHUNK)
+
+        def turn_back(s):
+            back = tps.tile([P, PACK, CHUNK], F32, name="back")
+            for t in range(PACK):
+                nc.tensor.transpose(back[:, t], zT[:, s, t], ident[:])
+            interleave(scopy, z_bf[:, span(s)], back[:])
+
+        def quantise_z(s):
+            quantise(z_codes[:, span(s)], z_scales[:, span(s)], z_bf[:, span(s)])
+
+        def finish(s, copy):
+            prod = tps.tile([P, N // P, CHUNK], F32, name="back")
+            for m in range(N // P):
+                mcols = slice(m * P, (m + 1) * P)
+                nc.tensor.matmul_mx(
+                    out=prod[:, m],
+                    lhsT=w2_codes[:, mcols].bitcast(FP8X4),
+                    lhsT_scale=w2_scales[:, mcols],
+                    rhs=z_codes[:, span(s)].bitcast(FP8X4),
+                    rhs_scale=z_scales[:, span(s)],
+                    start=True,
+                    stop=True,
+                )
+            res = ring.tile([P, N // P, CHUNK], F32, name="res")
+            copy(out=res[:], in_=prod[:])
+            nc.sync.dma_start(out=out[:, span(s)].rearrange("(m p) v -> p m v", p=P), in_=res[:])
+
+        for s in range(chunks):
+            g = ring.tile([P, D, CHUNK], F32, name="g_last")
+            for d in range(D):
+                gather(g, b, d, s * CHUNK, (s + 1) * CHUNK)
+            if s >= 1:
+                turn_back(s - 1)
+            bank = zps.tile([P, 1, P], F32, name="bank")
+            add_turned(bank[:, 0], g, 0)
+            scopy(out=zT[:, s, :, b * 32 : (b + 1) * 32], in_=bank[:, 0].rearrange("v (q t) -> v t q", t=PACK))
+            if s >= 2:
+                quantise_z(s - 2)
+                finish(s - 2, scopy)
+        quantise_z(chunks - 2)
+        turn_back(chunks - 1)
+        finish(chunks - 2, vcopy)
+        quantise_z(chunks - 1)
+        finish(chunks - 1, vcopy)

@@ -39,17 +39,15 @@ def tile_picked_gcn_mlp_none_sub_l_kernel(
 
     with ExitStack() as ctx:
         keep = ctx.enter_context(tc.tile_pool(name="keep", bufs=1))
-        ring = ctx.enter_context(tc.tile_pool(name="ring", bufs=2))
-        hps = ctx.enter_context(tc.psum_pool(name="hps", bufs=4))
-        zps = ctx.enter_context(tc.psum_pool(name="zps", bufs=2))
-        tps = ctx.enter_context(tc.psum_pool(name="tps", bufs=2))
+        ring = ctx.enter_context(tc.tile_pool(name="ring", bufs=3))
+        psum = ctx.enter_context(tc.psum_pool(name="psum", bufs=8))
 
         ident = keep.tile([P, P], F32, name="ident")
         make_identity(nc, ident[:])
 
         w1_raw = []
-        for b in range(BLOCKS):
-            w1_raw.append(keep.tile([P, PASSES, PACK, P], F32, name=f"w1_raw{b}"))
+        for b, width in ((0, P), (1, P), (2, 2 * P)):
+            w1_raw.append(keep.tile([P, PASSES, PACK, width], F32, name=f"w1_raw{b}"))
         x_raw = []
         for c in range(PASSES):
             x_raw.append(keep.tile([P, PACK, T], F32, name=f"x_raw{c}"))
@@ -59,11 +57,11 @@ def tile_picked_gcn_mlp_none_sub_l_kernel(
         gate_sb = keep.tile([P, D, V], F32, name="gate_sb")
         w2_raw = keep.tile([P, PACK, N], F32, name="w2_raw")
 
-        def load_w1(b):
+        def load_w1(b, width):
             for c in range(PASSES):
                 nc.sync.dma_start(
                     out=w1_raw[b][:, c],
-                    in_=w1[c * K_PASS : (c + 1) * K_PASS, b * P : (b + 1) * P].rearrange("(p j) n -> p j n", j=PACK),
+                    in_=w1[c * K_PASS : (c + 1) * K_PASS, b * P : b * P + width].rearrange("(p j) n -> p j n", j=PACK),
                 )
 
         def load_x(c, w0, w1_):
@@ -72,21 +70,20 @@ def tile_picked_gcn_mlp_none_sub_l_kernel(
                 in_=xT[c * K_PASS : (c + 1) * K_PASS, w0:w1_].rearrange("(p j) w -> p j w", j=PACK),
             )
 
-        pieces = [(0, 0, 512), (0, 512, 1024), (1, 0, 512), (1, 512, 1024), (2, 0, 512), (2, 512, 768), (2, 768, 1024)]
-        load_w1(0)
-        for c, a, e in pieces[:4]:
+        pieces = [(0, 0, 1024), (1, 0, 1024), (2, 0, 512), (2, 512, 768), (2, 768, 1024)]
+        load_w1(0, P)
+        for c, a, e in pieces[:2]:
             load_x(c, a, e)
         for tile, src in zip(lists, (pos1, pos2, pos3, pos4)):
             nc.sync.dma_start(tile[:], src)
-        for c, a, e in pieces[4:]:
+        for c, a, e in pieces[2:]:
             load_x(c, a, e)
         nc.sync.dma_start(out=gate_sb[:, 0], in_=gate[0])
         nc.sync.dma_start(out=gate_sb[:, 1], in_=gate[1])
-        load_w1(1)
+        load_w1(1, P)
         nc.sync.dma_start(out=gate_sb[:, 2], in_=gate[2])
         nc.sync.dma_start(out=gate_sb[:, 3], in_=gate[3])
-        load_w1(2)
-        load_w1(3)
+        load_w1(2, 2 * P)
         nc.sync.dma_start(out=w2_raw[:], in_=w2.rearrange("(p j) m -> p j m", j=PACK))
 
         x_bf, x_codes, x_scales = [], [], []
@@ -107,7 +104,8 @@ def tile_picked_gcn_mlp_none_sub_l_kernel(
 
         def interleave_w1(b, copy):
             for c in range(PASSES):
-                interleave(copy, w1_bf[b][:, c], w1_raw[b][:, c])
+                first = P if b == 3 else 0
+                interleave(copy, w1_bf[b][:, c], w1_raw[min(b, 2)][:, c, :, first : first + P])
 
         def quantise_w1(b, c0, c1):
             nc.vector.quantize_mx(
@@ -136,7 +134,7 @@ def tile_picked_gcn_mlp_none_sub_l_kernel(
         groups = ((0, 512), (512, 768), (768, 1024))
         accs = []
         for a, e in groups:
-            accs.append(hps.tile([P, HALF], F32, name="acc"))
+            accs.append(psum.tile([P, HALF], F32, name="bank"))
         for c, a, e in pieces:
             cut = a + (e - a) * 5 // 8
             interleave(vcopy, x_bf[c][:, a:cut], x_raw[c][:, :, a:cut])
@@ -173,29 +171,23 @@ def tile_picked_gcn_mlp_none_sub_l_kernel(
             offsets = lists[d][:, v0 // 16 : v1 // 16]
             nc.vector.tensor_tensor(g[:, d], h[b][:].indirect(offsets), gate_sb[:, d, v0:v1], MULT)
 
-        for b in range(BLOCKS - 1):
-            nb = b + 1
-            interleave_w1(nb, scopy)
-            g = ring.tile([P, D, V], F32, name="g")
-            acc_a = hps.tile([P, HALF], F32, name="acc")
-            acc_b = hps.tile([P, HALF], F32, name="acc")
-            gather(g, b, 0, 0, V)
-            quantise_w1(nb, 0, 2)
-            for c in range(2):
-                project(acc_a[:], nb, c, 0, HALF)
-                project(acc_b[:], nb, c, HALF, T)
-            gather(g, b, 1, 0, V)
-            quantise_w1(nb, 2, 3)
-            project(acc_a[:], nb, 2, 0, HALF)
-            project(acc_b[:], nb, 2, HALF, T)
-            scopy(out=h[nb][:, 0:HALF], in_=acc_a[:])
-            scopy(out=h[nb][:, HALF:T], in_=acc_b[:])
-            gather(g, b, 2, 0, V)
-            if nb == BLOCKS - 1:
-                interleave(scopy, w2_bf[:], w2_raw[:])
-                quantise(w2_codes[:], w2_scales[:], w2_bf[:])
-            gather(g, b, 3, 0, V)
-            bank = zps.tile([P, V // CHUNK, P], F32, name="bank")
+        def project_all(b, passes, pair):
+            for c in passes:
+                for half, acc in enumerate(pair):
+                    project(acc[:], b, c, half * HALF, (half + 1) * HALF)
+
+        def new_pair():
+            pair = []
+            for half in range(2):
+                pair.append(psum.tile([P, HALF], F32, name="bank"))
+            return pair
+
+        def bring(b, pair):
+            for half, acc in enumerate(pair):
+                scopy(out=h[b][:, half * HALF : (half + 1) * HALF], in_=acc[:])
+
+        def turn_block(b, g):
+            bank = psum.tile([P, V // CHUNK, P], F32, name="bank")
             for s in range(V // CHUNK):
                 add_turned(bank[:, s], g, s * CHUNK)
             scopy(
@@ -203,52 +195,109 @@ def tile_picked_gcn_mlp_none_sub_l_kernel(
                 in_=bank[:].rearrange("v s (q t) -> v s t q", t=PACK),
             )
 
-        b = BLOCKS - 1
-        chunks = V // CHUNK
+        gs = []
+        for b in range(BLOCKS - 1):
+            gs.append(ring.tile([P, D, V], F32, name="g"))
 
-        def span(s):
-            return slice(s * CHUNK, (s + 1) * CHUNK)
+        interleave_w1(1, scopy)
+        pair1 = new_pair()
+        gather(gs[0], 0, 0, 0, V)
+        quantise_w1(1, 0, 2)
+        project_all(1, (0, 1), pair1)
+        gather(gs[0], 0, 1, 0, V)
+        quantise_w1(1, 2, 3)
+        project_all(1, (2,), pair1)
+        bring(1, pair1)
+        gather(gs[0], 0, 2, 0, V)
+        gather(gs[0], 0, 3, 0, V)
+
+        interleave_w1(2, scopy)
+        pair2 = new_pair()
+        gather(gs[1], 1, 0, 0, V)
+        quantise_w1(2, 0, 2)
+        project_all(2, (0, 1), pair2)
+        gather(gs[1], 1, 1, 0, V)
+        quantise_w1(2, 2, 3)
+        project_all(2, (2,), pair2)
+        bring(2, pair2)
+        turn_block(0, gs[0])
+        gather(gs[1], 1, 2, 0, V)
+        interleave_w1(3, scopy)
+        gather(gs[1], 1, 3, 0, V)
+
+        pair3 = new_pair()
+        gather(gs[2], 2, 0, 0, V)
+        quantise_w1(3, 0, 2)
+        quantise_w1(3, 2, 3)
+        project_all(3, (0, 1, 2), pair3)
+        bring(3, pair3)
+        turn_block(1, gs[1])
+        gather(gs[2], 2, 1, 0, V)
+        interleave(scopy, w2_bf[:], w2_raw[:])
+        gather(gs[2], 2, 2, 0, V)
+        quantise(w2_codes[:], w2_scales[:], w2_bf[:])
+        gather(gs[2], 2, 3, 0, V)
+        turn_block(2, gs[2])
+
+        b = BLOCKS - 1
 
         def turn_back(s):
-            back = tps.tile([P, PACK, CHUNK], F32, name="back")
+            back = psum.tile([P, PACK, CHUNK], F32, name="bank")
             for t in range(PACK):
                 nc.tensor.transpose(back[:, t], zT[:, s, t], ident[:])
-            interleave(scopy, z_bf[:, span(s)], back[:])
+            interleave(scopy, z_bf[:, s * CHUNK : (s + 1) * CHUNK], back[:])
 
-        def quantise_z(s):
-            quantise(z_codes[:, span(s)], z_scales[:, span(s)], z_bf[:, span(s)])
+        def turn_back_last(s):
+            for first, copy in ((0, vcopy), (2, scopy)):
+                back = psum.tile([P, 2, CHUNK], F32, name="bank")
+                for t in range(2):
+                    nc.tensor.transpose(back[:, t], zT[:, s, first + t], ident[:])
+                interleave(copy, z_bf[:, s * CHUNK : (s + 1) * CHUNK, first : first + 2], back[:])
 
-        def finish(s, copy):
-            prod = tps.tile([P, N // P, CHUNK], F32, name="back")
+        def finish(v0, v1, copy):
+            quantise(z_codes[:, v0:v1], z_scales[:, v0:v1], z_bf[:, v0:v1])
+            prod = psum.tile([P, N // P, v1 - v0], F32, name="bank")
             for m in range(N // P):
                 mcols = slice(m * P, (m + 1) * P)
                 nc.tensor.matmul_mx(
                     out=prod[:, m],
                     lhsT=w2_codes[:, mcols].bitcast(FP8X4),
                     lhsT_scale=w2_scales[:, mcols],
-                    rhs=z_codes[:, span(s)].bitcast(FP8X4),
-                    rhs_scale=z_scales[:, span(s)],
+                    rhs=z_codes[:, v0:v1].bitcast(FP8X4),
+                    rhs_scale=z_scales[:, v0:v1],
                     start=True,
                     stop=True,
                 )
-            res = ring.tile([P, N // P, CHUNK], F32, name="res")
+            res = ring.tile([P, N // P, v1 - v0], F32, name="res")
             copy(out=res[:], in_=prod[:])
-            nc.sync.dma_start(out=out[:, span(s)].rearrange("(m p) v -> p m v", p=P), in_=res[:])
+            nc.sync.dma_start(out=out[:, v0:v1].rearrange("(m p) v -> p m v", p=P), in_=res[:])
 
-        for s in range(chunks):
-            g = ring.tile([P, D, CHUNK], F32, name="g_last")
+        def gather_chunk(v0, v1):
+            g = ring.tile([P, D, v1 - v0], F32, name="g_last")
             for d in range(D):
-                gather(g, b, d, s * CHUNK, (s + 1) * CHUNK)
-            if s >= 1:
-                turn_back(s - 1)
-            bank = zps.tile([P, 1, P], F32, name="bank")
-            add_turned(bank[:, 0], g, 0)
-            scopy(out=zT[:, s, :, b * 32 : (b + 1) * 32], in_=bank[:, 0].rearrange("v (q t) -> v t q", t=PACK))
-            if s >= 2:
-                quantise_z(s - 2)
-                finish(s - 2, scopy)
-        quantise_z(chunks - 2)
-        turn_back(chunks - 1)
-        finish(chunks - 2, vcopy)
-        quantise_z(chunks - 1)
-        finish(chunks - 1, vcopy)
+                gather(g, b, d, v0, v1)
+            return g
+
+        def turn_chunk(g, v0, v1):
+            subs = (v1 - v0) // CHUNK
+            bank = psum.tile([P, subs, P], F32, name="bank")
+            for s in range(subs):
+                add_turned(bank[:, s], g, s * CHUNK)
+            scopy(
+                out=zT[:, v0 // CHUNK : v1 // CHUNK, :, b * 32 : (b + 1) * 32],
+                in_=bank[:].rearrange("v s (q t) -> v s t q", t=PACK),
+            )
+
+        g_a = gather_chunk(0, 256)
+        turn_chunk(g_a, 0, 256)
+        g_b = gather_chunk(256, 384)
+        turn_back(0)
+        turn_back(1)
+        turn_chunk(g_b, 256, 384)
+        g_c = gather_chunk(384, 512)
+        turn_back(2)
+        turn_chunk(g_c, 384, 512)
+        finish(0, 256, scopy)
+        finish(256, 384, scopy)
+        turn_back_last(3)
+        finish(384, 512, vcopy)

@@ -86,32 +86,38 @@ def tile_picked_gcn_mlp_none_sub_l_kernel(
         load_w1(2, 2 * P)
         nc.sync.dma_start(out=w2_raw[:], in_=w2.rearrange("(p j) m -> p j m", j=PACK))
 
-        x_bf, x_codes, x_scales = [], [], []
+        x_codes, x_scales = [], []
         for c in range(PASSES):
-            x_bf.append(keep.tile([P, T, PACK], BF16, name=f"x_bf{c}", align_bytes=64))
             x_codes.append(keep.tile([P, T], U32, name=f"x_codes{c}", align_bytes=64))
             x_scales.append(keep.tile([P, T], U8, name=f"x_scales{c}", align_bytes=64))
-        w1_bf, w1_codes, w1_scales = [], [], []
+        def held(tag, shape, dtype):
+            return keep.tile(shape, dtype, name=tag, tag=tag, align_bytes=64)
+
+        x_bf = []
+        for i, (c, a, e) in enumerate(pieces):
+            x_bf.append(held(f"turn_{i - 3}" if i >= 3 else f"x_bf{i}", [P, e - a, PACK], BF16))
+        w1_codes, w1_scales = [], []
         for b in range(BLOCKS):
-            w1_bf.append(keep.tile([P, PASSES, P, PACK], BF16, name=f"w1_bf{b}", align_bytes=64))
-            w1_codes.append(keep.tile([P, PASSES, P], U32, name=f"w1_codes{b}", align_bytes=64))
-            w1_scales.append(keep.tile([P, PASSES, P], U8, name=f"w1_scales{b}", align_bytes=64))
+            w1_codes.append(held("turn_2" if b == 1 else f"w1_codes{b}", [P, PASSES, P], U32))
+            w1_scales.append(held("turn_3" if b == 1 else f"w1_scales{b}", [P, PASSES, P], U8))
 
         def quantise(codes, scales, grouped):
             nc.vector.quantize_mx(
                 out=codes.bitcast(FP8X4), scales=scales, in_=grouped.rearrange("p w t -> p (w t)")
             )
 
-        def interleave_w1(b, copy):
-            for c in range(PASSES):
-                first = P if b == 3 else 0
-                interleave(copy, w1_bf[b][:, c], w1_raw[min(b, 2)][:, c, :, first : first + P])
+        def group_w1(b, c0, c1, tag, copy):
+            grouped = held(tag, [P, c1 - c0, P, PACK], BF16)
+            first = P if b == 3 else 0
+            for c in range(c0, c1):
+                interleave(copy, grouped[:, c - c0], w1_raw[min(b, 2)][:, c, :, first : first + P])
+            return grouped
 
-        def quantise_w1(b, c0, c1):
+        def quantise_w1(b, c0, c1, grouped):
             nc.vector.quantize_mx(
                 out=w1_codes[b][:, c0:c1].rearrange("p c n -> p (c n)").bitcast(FP8X4),
                 scales=w1_scales[b][:, c0:c1].rearrange("p c n -> p (c n)"),
-                in_=w1_bf[b][:, c0:c1].rearrange("p c n t -> p (c n t)"),
+                in_=grouped[:].rearrange("p c n t -> p (c n t)"),
             )
 
         def project(acc, b, c, a, e):
@@ -125,9 +131,10 @@ def tile_picked_gcn_mlp_none_sub_l_kernel(
                 stop=(c == PASSES - 1),
             )
 
-        interleave_w1(0, vcopy)
-        quantise_w1(0, 0, 2)
-        quantise_w1(0, 2, 3)
+        w1_bf0a = group_w1(0, 0, 2, "w1_bf0a", vcopy)
+        quantise_w1(0, 0, 2, w1_bf0a)
+        w1_bf0b = group_w1(0, 2, 3, "w1_bf0b", vcopy)
+        quantise_w1(0, 2, 3, w1_bf0b)
         h = []
         for b in range(BLOCKS):
             h.append(keep.tile([P, T], F32, name=f"h{b}"))
@@ -135,11 +142,11 @@ def tile_picked_gcn_mlp_none_sub_l_kernel(
         accs = []
         for a, e in groups:
             accs.append(psum.tile([P, HALF], F32, name="bank"))
-        for c, a, e in pieces:
-            cut = a + (e - a) * 5 // 8
-            interleave(vcopy, x_bf[c][:, a:cut], x_raw[c][:, :, a:cut])
-            interleave(scopy, x_bf[c][:, cut:e], x_raw[c][:, :, cut:e])
-            quantise(x_codes[c][:, a:e], x_scales[c][:, a:e], x_bf[c][:, a:e])
+        for grouped, (c, a, e) in zip(x_bf, pieces):
+            cut = (e - a) * 5 // 8 if e - a > 256 else 192
+            interleave(vcopy, grouped[:, 0:cut], x_raw[c][:, :, a : a + cut])
+            interleave(scopy, grouped[:, cut : e - a], x_raw[c][:, :, a + cut : e])
+            quantise(x_codes[c][:, a:e], x_scales[c][:, a:e], grouped[:])
             for acc, (ga, ge) in zip(accs, groups):
                 if a <= ga and ge <= e:
                     project(acc[:, 0 : ge - ga], 0, c, ga, ge)
@@ -147,29 +154,20 @@ def tile_picked_gcn_mlp_none_sub_l_kernel(
         scopy(out=h[0][:, 512:768], in_=accs[1][:, 0:256])
         vcopy(out=h[0][:, 768:1024], in_=accs[2][:, 0:256])
 
-        w2_bf = keep.tile([P, N, PACK], BF16, name="w2_bf", align_bytes=64)
         w2_codes = keep.tile([P, N], U32, name="w2_codes", align_bytes=64)
         w2_scales = keep.tile([P, N], U8, name="w2_scales", align_bytes=64)
 
-        zT = keep.tile([P, V // CHUNK, PACK, P], F32, name="zT")
+        zT = keep.tile([P, V // CHUNK, 2, P, 2], BF16, name="zT", align_bytes=64)
         z_bf = keep.tile([P, V, PACK], BF16, name="z_bf", align_bytes=64)
+        z_words = z_bf[:].bitcast(F32)
         z_codes = keep.tile([P, V], U32, name="z_codes", align_bytes=64)
         z_scales = keep.tile([P, V], U8, name="z_scales", align_bytes=64)
 
-        def add_turned(dst, g, first):
-            for d in range(D):
-                nc.tensor.matmul(
-                    dst,
-                    g[:, d, first : first + CHUNK],
-                    ident[:],
-                    start=(d == 0),
-                    stop=(d == D - 1),
-                    is_transpose=True,
-                )
-
-        def gather(g, b, d, v0, v1):
+        def gather(b, d, v0, v1, tag):
+            g = held(tag, [P, v1 - v0], F32)
             offsets = lists[d][:, v0 // 16 : v1 // 16]
-            nc.vector.tensor_tensor(g[:, d], h[b][:].indirect(offsets), gate_sb[:, d, v0:v1], MULT)
+            nc.vector.tensor_tensor(g[:], h[b][:].indirect(offsets), gate_sb[:, d, v0:v1], MULT)
+            return g
 
         def project_all(b, passes, pair):
             for c in passes:
@@ -186,81 +184,116 @@ def tile_picked_gcn_mlp_none_sub_l_kernel(
             for half, acc in enumerate(pair):
                 scopy(out=h[b][:, half * HALF : (half + 1) * HALF], in_=acc[:])
 
-        def turn_block(b, g):
-            bank = psum.tile([P, V // CHUNK, P], F32, name="bank")
-            for s in range(V // CHUNK):
-                add_turned(bank[:, s], g, s * CHUNK)
-            scopy(
-                out=zT[:, :, :, b * 32 : (b + 1) * 32],
-                in_=bank[:].rearrange("v s (q t) -> v s t q", t=PACK),
-            )
+        def turn(b, g, v0, v1):
+            subs = (v1 - v0) // CHUNK
+            bank = psum.tile([P, subs, P], F32, name="bank")
+            for s in range(subs):
+                for d in range(D):
+                    nc.tensor.matmul(
+                        bank[:, s],
+                        g[d][:, s * CHUNK : (s + 1) * CHUNK],
+                        ident[:],
+                        start=(d == 0),
+                        stop=(d == D - 1),
+                        is_transpose=True,
+                    )
+            by_pair = bank[:].rearrange("v s (q u e) -> v s u q e", u=2, e=2)
+            for u in range(2):
+                scopy(
+                    out=zT[:, v0 // CHUNK : v1 // CHUNK, u, b * 32 : (b + 1) * 32],
+                    in_=by_pair[:, :, u],
+                )
 
-        gs = []
-        for b in range(BLOCKS - 1):
-            gs.append(ring.tile([P, D, V], F32, name="g"))
-
-        interleave_w1(1, scopy)
+        w1_bf1a = group_w1(1, 0, 2, "turn_1", scopy)
+        w1_bf1b = group_w1(1, 2, 3, "turn_0", scopy)
         pair1 = new_pair()
-        gather(gs[0], 0, 0, 0, V)
-        quantise_w1(1, 0, 2)
+        g00 = gather(0, 0, 0, V, "g00")
+        quantise_w1(1, 0, 2, w1_bf1a)
         project_all(1, (0, 1), pair1)
-        gather(gs[0], 0, 1, 0, V)
-        quantise_w1(1, 2, 3)
+        g01 = gather(0, 1, 0, V, "turn_1")
+        quantise_w1(1, 2, 3, w1_bf1b)
         project_all(1, (2,), pair1)
         bring(1, pair1)
-        gather(gs[0], 0, 2, 0, V)
-        gather(gs[0], 0, 3, 0, V)
+        g02 = gather(0, 2, 0, V, "turn_0")
+        g03 = gather(0, 3, 0, V, "g03")
 
-        interleave_w1(2, scopy)
+        w1_bf2a = group_w1(2, 0, 2, "turn_2", scopy)
+        w1_bf2b = group_w1(2, 2, 3, "turn_3", scopy)
         pair2 = new_pair()
-        gather(gs[1], 1, 0, 0, V)
-        quantise_w1(2, 0, 2)
+        g10 = gather(1, 0, 0, V, "g10")
+        quantise_w1(2, 0, 2, w1_bf2a)
         project_all(2, (0, 1), pair2)
-        gather(gs[1], 1, 1, 0, V)
-        quantise_w1(2, 2, 3)
+        g11 = gather(1, 1, 0, V, "turn_2")
+        quantise_w1(2, 2, 3, w1_bf2b)
         project_all(2, (2,), pair2)
+        w1_bf3a = group_w1(3, 0, 2, "turn_4", scopy)
+        w1_bf3b = group_w1(3, 2, 3, "turn_5", scopy)
         bring(2, pair2)
-        turn_block(0, gs[0])
-        gather(gs[1], 1, 2, 0, V)
-        interleave_w1(3, scopy)
-        gather(gs[1], 1, 3, 0, V)
+        g12 = gather(1, 2, 0, V, "turn_3")
+        g13 = gather(1, 3, 0, V, "g13")
 
         pair3 = new_pair()
-        gather(gs[2], 2, 0, 0, V)
-        quantise_w1(3, 0, 2)
-        quantise_w1(3, 2, 3)
-        project_all(3, (0, 1, 2), pair3)
-        bring(3, pair3)
-        turn_block(1, gs[1])
-        gather(gs[2], 2, 1, 0, V)
+        quantise_w1(3, 0, 2, w1_bf3a)
+        project_all(3, (0, 1), pair3)
+        g20 = gather(2, 0, 0, V, "turn_4")
+        quantise_w1(3, 2, 3, w1_bf3b)
+        project_all(3, (2,), pair3)
+        w2_bf = held("turn_6", [P, N, PACK], BF16)
         interleave(scopy, w2_bf[:], w2_raw[:])
-        gather(gs[2], 2, 2, 0, V)
+        bring(3, pair3)
+        turn(0, (g00, g01, g02, g03), 0, V)
+        g21 = gather(2, 1, 0, V, "turn_5")
         quantise(w2_codes[:], w2_scales[:], w2_bf[:])
-        gather(gs[2], 2, 3, 0, V)
-        turn_block(2, gs[2])
+        turn(1, (g10, g11, g12, g13), 0, V)
+        g22 = gather(2, 2, 0, V, "turn_6")
+        g23 = gather(2, 3, 0, V, "g23")
+        turn(2, (g20, g21, g22, g23), 0, V)
 
-        b = BLOCKS - 1
+        def last_chunk(v0, v1):
+            subs = range(v0 // CHUNK, v1 // CHUNK)
+            banks = []
+            for s in subs:
+                banks.append(psum.tile([P, P], F32, name="bank"))
+            for d in range(D):
+                g = gather(BLOCKS - 1, d, v0, v1, f"last_{v0}_{d}")
+                for s, bank in zip(subs, banks):
+                    nc.tensor.matmul(
+                        bank[:],
+                        g[:, s * CHUNK - v0 : (s + 1) * CHUNK - v0],
+                        ident[:],
+                        start=(d == 0),
+                        stop=(d == D - 1),
+                        is_transpose=True,
+                    )
+            for s, bank in zip(subs, banks):
+                scopy(
+                    out=zT[:, s, :, (BLOCKS - 1) * 32 : BLOCKS * 32],
+                    in_=bank[:].rearrange("v (q u e) -> v u q e", u=2, e=2),
+                )
+
+        def back_words(dst, s, u):
+            nc.tensor.transpose(dst, zT[:, s, u].rearrange("v p e -> v (p e)").bitcast(F32), ident[:])
 
         def turn_back(s):
-            back = psum.tile([P, PACK, CHUNK], F32, name="bank")
-            for t in range(PACK):
-                nc.tensor.transpose(back[:, t], zT[:, s, t], ident[:])
-            interleave(scopy, z_bf[:, s * CHUNK : (s + 1) * CHUNK], back[:])
+            back = psum.tile([P, 2, CHUNK], F32, name="bank")
+            for u in range(2):
+                back_words(back[:, u], s, u)
+            interleave(scopy, z_words[:, s * CHUNK : (s + 1) * CHUNK], back[:])
 
         def turn_back_last(s):
-            for first, copy in ((0, vcopy), (2, scopy)):
-                back = psum.tile([P, 2, CHUNK], F32, name="bank")
-                for t in range(2):
-                    nc.tensor.transpose(back[:, t], zT[:, s, first + t], ident[:])
-                interleave(copy, z_bf[:, s * CHUNK : (s + 1) * CHUNK, first : first + 2], back[:])
+            for u, copy in ((0, vcopy), (1, scopy)):
+                back = psum.tile([P, CHUNK], F32, name="bank")
+                back_words(back[:], s, u)
+                copy(out=z_words[:, s * CHUNK : (s + 1) * CHUNK, u], in_=back[:])
 
-        def finish(v0, v1, copy):
+        def finish(v0, v1, copies):
             quantise(z_codes[:, v0:v1], z_scales[:, v0:v1], z_bf[:, v0:v1])
-            prod = psum.tile([P, N // P, v1 - v0], F32, name="bank")
-            for m in range(N // P):
+            res = ring.tile([P, N // P, v1 - v0], F32, name="res")
+            for m, copy in enumerate(copies):
+                prod = psum.tile([P, v1 - v0], F32, name="bank")
                 mcols = slice(m * P, (m + 1) * P)
                 nc.tensor.matmul_mx(
-                    out=prod[:, m],
+                    out=prod[:],
                     lhsT=w2_codes[:, mcols].bitcast(FP8X4),
                     lhsT_scale=w2_scales[:, mcols],
                     rhs=z_codes[:, v0:v1].bitcast(FP8X4),
@@ -268,36 +301,16 @@ def tile_picked_gcn_mlp_none_sub_l_kernel(
                     start=True,
                     stop=True,
                 )
-            res = ring.tile([P, N // P, v1 - v0], F32, name="res")
-            copy(out=res[:], in_=prod[:])
+                copy(out=res[:, m], in_=prod[:])
             nc.sync.dma_start(out=out[:, v0:v1].rearrange("(m p) v -> p m v", p=P), in_=res[:])
 
-        def gather_chunk(v0, v1):
-            g = ring.tile([P, D, v1 - v0], F32, name="g_last")
-            for d in range(D):
-                gather(g, b, d, v0, v1)
-            return g
-
-        def turn_chunk(g, v0, v1):
-            subs = (v1 - v0) // CHUNK
-            bank = psum.tile([P, subs, P], F32, name="bank")
-            for s in range(subs):
-                add_turned(bank[:, s], g, s * CHUNK)
-            scopy(
-                out=zT[:, v0 // CHUNK : v1 // CHUNK, :, b * 32 : (b + 1) * 32],
-                in_=bank[:].rearrange("v s (q t) -> v s t q", t=PACK),
-            )
-
-        g_a = gather_chunk(0, 256)
-        turn_chunk(g_a, 0, 256)
-        g_b = gather_chunk(256, 384)
+        last_chunk(0, 256)
+        last_chunk(256, 384)
         turn_back(0)
         turn_back(1)
-        turn_chunk(g_b, 256, 384)
-        g_c = gather_chunk(384, 512)
+        last_chunk(384, 512)
         turn_back(2)
-        turn_chunk(g_c, 384, 512)
-        finish(0, 256, scopy)
-        finish(256, 384, scopy)
         turn_back_last(3)
-        finish(384, 512, vcopy)
+        finish(0, 256, (vcopy, scopy))
+        finish(256, 384, (vcopy, scopy))
+        finish(384, 512, (vcopy, scopy))

from contextlib import ExitStack

import concourse.mybir as mybir
from concourse.masks import make_identity

F32 = mybir.dt.float32
BF16 = mybir.dt.bfloat16
U32 = mybir.dt.uint32
U16 = mybir.dt.uint16
U8 = mybir.dt.uint8
FP8X4 = mybir.dt.float8_e4m3fn_x4
MULT = mybir.AluOpType.mult

P = 128
PACK = 4
K, T, D, V, H, N = 1536, 1024, 4, 512, 512, 256
K_PASS = P * PACK
PASSES = K // K_PASS
BLOCKS = H // P
HALF = 512
CHUNK = 128

FLOPS = 2 * (K * H * T + H * N * V)


def interleave(copy, dst, src):
    copy(
        out=dst.rearrange("p (c i) t -> p c t i", i=4),
        in_=src.rearrange("p t (c i) -> p c t i", i=4),
    )


def tile_picked_gcn_mlp_none_sub_l_kernel(
    tc, xT, w1, w2, gate, pos1, pos2, pos3, pos4, out
):
    nc = tc.nc
    vcopy = nc.vector.tensor_copy
    scopy = nc.scalar.copy

    with ExitStack() as ctx:
        keep = ctx.enter_context(tc.tile_pool(name="keep", bufs=1))
        ring = ctx.enter_context(tc.tile_pool(name="ring", bufs=3))
        psum = ctx.enter_context(tc.psum_pool(name="psum", bufs=8))

        ident = keep.tile([P, P], F32, name="ident")
        make_identity(nc, ident[:])

        w1_raw = []
        for b, width in ((0, P), (1, P), (2, 2 * P)):
            w1_raw.append(keep.tile([P, PASSES, PACK, width], F32, name=f"w1_raw{b}"))
        x_raw = []
        for c in range(PASSES):
            x_raw.append(keep.tile([P, PACK, T], F32, name=f"x_raw{c}"))
        lists = []
        for d in range(D):
            lists.append(keep.tile([P, V // 16], U16, name=f"list{d}"))
        gate_sb = keep.tile([P, D, V], F32, name="gate_sb")
        w2_raw = keep.tile([P, PACK, N], F32, name="w2_raw")

        def load_w1(b, width):
            for c in range(PASSES):
                nc.sync.dma_start(
                    out=w1_raw[b][:, c],
                    in_=w1[c * K_PASS : (c + 1) * K_PASS, b * P : b * P + width].rearrange("(p j) n -> p j n", j=PACK),
                )

        def load_x(c, w0, w1_):
            nc.sync.dma_start(
                out=x_raw[c][:, :, w0:w1_],
                in_=xT[c * K_PASS : (c + 1) * K_PASS, w0:w1_].rearrange("(p j) w -> p j w", j=PACK),
            )

        pieces = [(0, 0, 1024), (1, 0, 1024), (2, 0, 512), (2, 512, 768), (2, 768, 1024)]
        load_w1(0, P)
        for c, a, e in pieces[:2]:
            load_x(c, a, e)
        for tile, src in zip(lists, (pos1, pos2, pos3, pos4)):
            nc.sync.dma_start(tile[:], src)
        for c, a, e in pieces[2:]:
            load_x(c, a, e)
        nc.sync.dma_start(out=gate_sb[:, 0], in_=gate[0])
        nc.sync.dma_start(out=gate_sb[:, 1], in_=gate[1])
        load_w1(1, P)
        nc.sync.dma_start(out=gate_sb[:, 2], in_=gate[2])
        nc.sync.dma_start(out=gate_sb[:, 3], in_=gate[3])
        load_w1(2, 2 * P)
        nc.sync.dma_start(out=w2_raw[:], in_=w2.rearrange("(p j) m -> p j m", j=PACK))

        x_codes, x_scales = [], []
        for c in range(PASSES):
            x_codes.append(keep.tile([P, T], U32, name=f"x_codes{c}", align_bytes=64))
            x_scales.append(keep.tile([P, T], U8, name=f"x_scales{c}", align_bytes=64))
        def held(tag, shape, dtype):
            return keep.tile(shape, dtype, name=tag, tag=tag, align_bytes=64)

        x_bf = []
        for i, (c, a, e) in enumerate(pieces):
            x_bf.append(held(f"turn_{i - 3}" if i >= 3 else f"x_bf{i}", [P, e - a, PACK], BF16))
        w1_codes, w1_scales = [], []
        for b in range(BLOCKS):
            w1_codes.append(held("turn_2" if b == 1 else f"w1_codes{b}", [P, PASSES, P], U32))
            w1_scales.append(held("turn_3" if b == 1 else f"w1_scales{b}", [P, PASSES, P], U8))

        def quantise(codes, scales, grouped):
            nc.vector.quantize_mx(
                out=codes.bitcast(FP8X4), scales=scales, in_=grouped.rearrange("p w t -> p (w t)")
            )

        def group_w1(b, c0, c1, tag, copy):
            grouped = held(tag, [P, c1 - c0, P, PACK], BF16)
            first = P if b == 3 else 0
            for c in range(c0, c1):
                interleave(copy, grouped[:, c - c0], w1_raw[min(b, 2)][:, c, :, first : first + P])
            return grouped

        def quantise_w1(b, c0, c1, grouped):
            nc.vector.quantize_mx(
                out=w1_codes[b][:, c0:c1].rearrange("p c n -> p (c n)").bitcast(FP8X4),
                scales=w1_scales[b][:, c0:c1].rearrange("p c n -> p (c n)"),
                in_=grouped[:].rearrange("p c n t -> p (c n t)"),
            )

        def project(acc, b, c, a, e):
            nc.tensor.matmul_mx(
                out=acc,
                lhsT=w1_codes[b][:, c].bitcast(FP8X4),
                lhsT_scale=w1_scales[b][:, c],
                rhs=x_codes[c][:, a:e].bitcast(FP8X4),
                rhs_scale=x_scales[c][:, a:e],
                start=(c == 0),
                stop=(c == PASSES - 1),
            )

        w1_bf0a = group_w1(0, 0, 2, "w1_bf0a", vcopy)
        quantise_w1(0, 0, 2, w1_bf0a)
        w1_bf0b = group_w1(0, 2, 3, "w1_bf0b", vcopy)
        quantise_w1(0, 2, 3, w1_bf0b)
        h = []
        for b in range(BLOCKS):
            h.append(keep.tile([P, T], F32, name=f"h{b}"))
        groups = ((0, 512), (512, 768), (768, 1024))
        accs = []
        for a, e in groups:
            accs.append(psum.tile([P, HALF], F32, name="bank"))
        for grouped, (c, a, e) in zip(x_bf, pieces):
            cut = (e - a) * 5 // 8 if e - a > 256 else 192
            interleave(vcopy, grouped[:, 0:cut], x_raw[c][:, :, a : a + cut])
            interleave(scopy, grouped[:, cut : e - a], x_raw[c][:, :, a + cut : e])
            quantise(x_codes[c][:, a:e], x_scales[c][:, a:e], grouped[:])
            for acc, (ga, ge) in zip(accs, groups):
                if a <= ga and ge <= e:
                    project(acc[:, 0 : ge - ga], 0, c, ga, ge)
        scopy(out=h[0][:, 0:512], in_=accs[0][:])
        scopy(out=h[0][:, 512:768], in_=accs[1][:, 0:256])
        vcopy(out=h[0][:, 768:1024], in_=accs[2][:, 0:256])

        w2_codes = keep.tile([P, N], U32, name="w2_codes", align_bytes=64)
        w2_scales = keep.tile([P, N], U8, name="w2_scales", align_bytes=64)

        zT = keep.tile([P, V // CHUNK, 2, P, 2], BF16, name="zT", align_bytes=64)
        z_bf = keep.tile([P, V, PACK], BF16, name="z_bf", align_bytes=64)
        z_words = z_bf[:].bitcast(F32)
        z_codes = keep.tile([P, V], U32, name="z_codes", align_bytes=64)
        z_scales = keep.tile([P, V], U8, name="z_scales", align_bytes=64)

        def gather(b, d, v0, v1, tag):
            g = held(tag, [P, v1 - v0], F32)
            offsets = lists[d][:, v0 // 16 : v1 // 16]
            nc.vector.tensor_tensor(g[:], h[b][:].indirect(offsets), gate_sb[:, d, v0:v1], MULT)
            return g

        def project_all(b, passes, pair):
            for c in passes:
                for half, acc in enumerate(pair):
                    project(acc[:], b, c, half * HALF, (half + 1) * HALF)

        def new_pair():
            pair = []
            for half in range(2):
                pair.append(psum.tile([P, HALF], F32, name="bank"))
            return pair

        def bring(b, pair):
            for half, acc in enumerate(pair):
                scopy(out=h[b][:, half * HALF : (half + 1) * HALF], in_=acc[:])

        def turn(b, g, v0, v1):
            subs = (v1 - v0) // CHUNK
            bank = psum.tile([P, subs, P], F32, name="bank")
            for s in range(subs):
                for d in range(D):
                    nc.tensor.matmul(
                        bank[:, s],
                        g[d][:, s * CHUNK : (s + 1) * CHUNK],
                        ident[:],
                        start=(d == 0),
                        stop=(d == D - 1),
                        is_transpose=True,
                    )
            by_pair = bank[:].rearrange("v s (q u e) -> v s u q e", u=2, e=2)
            for u in range(2):
                scopy(
                    out=zT[:, v0 // CHUNK : v1 // CHUNK, u, b * 32 : (b + 1) * 32],
                    in_=by_pair[:, :, u],
                )

        w1_bf1a = group_w1(1, 0, 2, "turn_1", scopy)
        w1_bf1b = group_w1(1, 2, 3, "turn_0", scopy)
        pair1 = new_pair()
        g00 = gather(0, 0, 0, V, "g00")
        quantise_w1(1, 0, 2, w1_bf1a)
        project_all(1, (0, 1), pair1)
        g01 = gather(0, 1, 0, V, "turn_1")
        quantise_w1(1, 2, 3, w1_bf1b)
        project_all(1, (2,), pair1)
        bring(1, pair1)
        g02 = gather(0, 2, 0, V, "turn_0")
        g03 = gather(0, 3, 0, V, "g03")

        w1_bf2a = group_w1(2, 0, 2, "turn_2", scopy)
        w1_bf2b = group_w1(2, 2, 3, "turn_3", scopy)
        pair2 = new_pair()
        g10 = gather(1, 0, 0, V, "g10")
        quantise_w1(2, 0, 2, w1_bf2a)
        project_all(2, (0, 1), pair2)
        g11 = gather(1, 1, 0, V, "turn_2")
        quantise_w1(2, 2, 3, w1_bf2b)
        project_all(2, (2,), pair2)
        w1_bf3a = group_w1(3, 0, 2, "turn_4", scopy)
        w1_bf3b = group_w1(3, 2, 3, "turn_5", scopy)
        bring(2, pair2)
        g12 = gather(1, 2, 0, V, "turn_3")
        g13 = gather(1, 3, 0, V, "g13")

        pair3 = new_pair()
        quantise_w1(3, 0, 2, w1_bf3a)
        project_all(3, (0, 1), pair3)
        g20 = gather(2, 0, 0, V, "turn_4")
        quantise_w1(3, 2, 3, w1_bf3b)
        project_all(3, (2,), pair3)
        w2_bf = held("turn_6", [P, N, PACK], BF16)
        interleave(scopy, w2_bf[:], w2_raw[:])
        bring(3, pair3)
        turn(0, (g00, g01, g02, g03), 0, V)
        g21 = gather(2, 1, 0, V, "turn_5")
        quantise(w2_codes[:], w2_scales[:], w2_bf[:])
        turn(1, (g10, g11, g12, g13), 0, V)
        g22 = gather(2, 2, 0, V, "turn_6")
        g23 = gather(2, 3, 0, V, "g23")
        turn(2, (g20, g21, g22, g23), 0, V)

        def last_chunk(v0, v1):
            subs = range(v0 // CHUNK, v1 // CHUNK)
            banks = []
            for s in subs:
                banks.append(psum.tile([P, P], F32, name="bank"))
            for d in range(D):
                g = gather(BLOCKS - 1, d, v0, v1, f"last_{v0}_{d}")
                for s, bank in zip(subs, banks):
                    nc.tensor.matmul(
                        bank[:],
                        g[:, s * CHUNK - v0 : (s + 1) * CHUNK - v0],
                        ident[:],
                        start=(d == 0),
                        stop=(d == D - 1),
                        is_transpose=True,
                    )
            for s, bank in zip(subs, banks):
                scopy(
                    out=zT[:, s, :, (BLOCKS - 1) * 32 : BLOCKS * 32],
                    in_=bank[:].rearrange("v (q u e) -> v u q e", u=2, e=2),
                )

        def back_words(dst, s, u):
            nc.tensor.transpose(dst, zT[:, s, u].rearrange("v p e -> v (p e)").bitcast(F32), ident[:])

        def turn_back(s):
            back = psum.tile([P, 2, CHUNK], F32, name="bank")
            for u in range(2):
                back_words(back[:, u], s, u)
            interleave(scopy, z_words[:, s * CHUNK : (s + 1) * CHUNK], back[:])

        def turn_back_last(s):
            for u, copy in ((0, vcopy), (1, scopy)):
                back = psum.tile([P, CHUNK], F32, name="bank")
                back_words(back[:], s, u)
                copy(out=z_words[:, s * CHUNK : (s + 1) * CHUNK, u], in_=back[:])

        def finish(v0, v1, copies):
            quantise(z_codes[:, v0:v1], z_scales[:, v0:v1], z_bf[:, v0:v1])
            res = ring.tile([P, N // P, v1 - v0], F32, name="res")
            for m, copy in enumerate(copies):
                prod = psum.tile([P, v1 - v0], F32, name="bank")
                mcols = slice(m * P, (m + 1) * P)
                nc.tensor.matmul_mx(
                    out=prod[:],
                    lhsT=w2_codes[:, mcols].bitcast(FP8X4),
                    lhsT_scale=w2_scales[:, mcols],
                    rhs=z_codes[:, v0:v1].bitcast(FP8X4),
                    rhs_scale=z_scales[:, v0:v1],
                    start=True,
                    stop=True,
                )
                copy(out=res[:, m], in_=prod[:])
            nc.sync.dma_start(out=out[:, v0:v1].rearrange("(m p) v -> p m v", p=P), in_=res[:])

        last_chunk(0, 256)
        last_chunk(256, 384)
        turn_back(0)
        turn_back(1)
        last_chunk(384, 512)
        turn_back(2)
        turn_back_last(3)
        finish(0, 256, (vcopy, scopy))
        finish(256, 384, (vcopy, scopy))
        finish(384, 512, (vcopy, scopy))
